import numpy as np, ml_dtypes
CORES = [35,38,43,46]
N = 4
import mx_ref
BF = ml_dtypes.bfloat16
def rowtile(v, k):
    z = np.concatenate([v, np.zeros((1, v.shape[1]), BF)])
    return np.concatenate([np.ascontiguousarray(z[k[:, 4 * m:4 * m + 4]].transpose(0, 2, 1)).reshape(128, -1) for m in range(k.shape[1] // 4)], axis=1)
def cut(t, i, w=512):
    return t[:, w * i:w * i + w]
def f(rng, *shape):
    return mx_ref.flush((rng.standard_normal(shape, dtype=np.float32) * np.exp2(rng.integers(-2, 3, shape[:-1] + (1,)))).astype(BF))
def wide(rng, *shape, cols=0):
    v = rng.standard_normal(shape, dtype=np.float32) * np.exp2(rng.integers(-12, 13, shape)).astype(np.float32)
    if cols: v *= np.repeat(np.exp2(rng.integers(-cols, cols + 1, shape[:-2] + (1, shape[-1] // 4))) * (rng.random(shape[:-2] + (1, shape[-1] // 4)) > 0.0625), 4, axis=-1).astype(np.float32)
    return mx_ref.flush(v.astype(BF))
T, GW, CAPP = 1024, 1024, 256
def counts(rng):
    n = rng.integers(0, CAPP + 1, (N, N))
    for e in range(N):
        if n[:, e].sum() < CAPP: n[rng.integers(0, N), e] = CAPP
    return n
def lists(rng, n):
    l = np.full((N, N, 512), -1)
    for s in range(N):
        for e in range(N): l[s, e, :n[s, e]] = rng.integers(0, T, n[s, e])
    return l
def store(l):
    return np.ascontiguousarray(l.reshape(N, N, 128, 4).transpose(0, 2, 1, 3)).reshape(N, 128, 4 * N).astype(np.int32)
def setup_inputs(rng):
    return {"x": f(rng, N, T, 128), "dy": f(rng, N, T, GW), "pick": store(lists(rng, counts(rng)))}
def setup_inputs_alike(rng):
    d = setup_inputs(rng); l = np.full((N, N, 512), -1); n = rng.integers(CAPP // 2, CAPP + 1)
    l[:, :, :n] = rng.integers(0, T, n)
    d["pick"] = store(l); return d
def setup_inputs_counts(rng):
    d = setup_inputs(rng)
    n = np.array([0, 1, 33, CAPP])[(np.arange(N)[:, None] + np.arange(N) + rng.integers(0, 4)) % 4][rng.permutation(N)]
    d["pick"] = store(lists(rng, n)); return d
def setup_inputs_giant(rng):
    d = setup_inputs(rng); l = lists(rng, rng.integers(64, CAPP + 1, (N, N)))
    for s in range(N):
        k = rng.permutation(T); kx, kg = k[:T // 32], k[T // 32:T // 16]
        d["x"][s, kx] = (d["x"][s, kx].astype(np.float32) * np.float32(4096)).astype(BF)
        d["dy"][s, kg] = (d["dy"][s, kg].astype(np.float32) * np.float32(4096)).astype(BF)
        for e in range(N):
            i = rng.permutation(32)
            l[s, e, i[0]], l[s, e, i[1]] = rng.choice(kx), rng.choice(kg)
    d["pick"] = store(l); return d
def setup_inputs_reversed(rng):
    d = setup_inputs(rng); n = counts(rng); l = lists(rng, n)
    for s in range(N):
        for e in range(N): l[s, e, :n[s, e]] = np.sort(l[s, e, :n[s, e]])[::-1]
    d["pick"] = store(l); return d
def setup_inputs_spread(rng):
    d = setup_inputs(rng); d["x"] = wide(rng, N, T, 128); d["dy"] = wide(rng, N, T, GW)
    d["pick"] = store(lists(rng, rng.integers(CAPP // 2, CAPP + 1, (N, N)))); return d
def check_inputs(d):
    b = []
    for q in ("x", "dy"):
        v = np.abs(np.asarray(d[q]).astype(np.float32))
        if not np.isfinite(v).all() or ((v != 0) & ((v < 2.0 ** -30) | (v > 2.0 ** 30))).any(): b.append(q)
    for s in range(N):
        for e in range(N):
            k = np.asarray(d["pick"][s])[:, 4 * e:4 * e + 4].reshape(-1); n = int((k >= 0).sum())
            if n > CAPP or k.max() >= T or (k[:n] < 0).any() or (k[n:] != -1).any(): b.append("pick")
    return b
def reference(x, dy, pick):
    y = np.zeros((N, 128, GW), np.float32)
    for e in range(N):
        for s in range(N):
            k = pick[s][:, 4 * e:4 * e + 4]
            X, G = mx_ref.quantize(rowtile(x[s], k)), rowtile(dy[s], k)
            for i in range(GW // 512): y[e][:, 512 * i:512 * i + 512] += mx_ref.matmul(X, mx_ref.quantize(cut(G, i, 2048)))
    return {"y": y}

from concourse.bass import IndirectOffsetOnAxis
from concourse.mybir import dt, ActivationFunctionType

N = 4
ROWS, XW, GW, HALF = 1024, 128, 1024, 512
RW = GW + XW
W = 2 * XW + HALF
G0, X1 = XW, XW + HALF

SCRATCH = {
    "xd": ("dram", [ROWS, RW], "bfloat16"),
    "idx": ("sbuf", [128, 16], "int32"),
    "p0": ("psum", [128, 512], "float32"),
    "p1": ("psum", [128, 512], "float32"),
    "o0": ("sbuf", [128, 512], "float32"),
    "o1": ("sbuf", [128, 512], "float32"),
}
for _k in range(N):
    for _u in range(2):
        SCRATCH["dg%d%d" % (_k, _u)] = ("sbuf", [128, RW], "bfloat16")
    SCRATCH["tile%d" % _k] = ("sbuf", [128, 4 * W], "bfloat16")
    SCRATCH["qc%d" % _k] = ("sbuf", [128, W], "float8_e4m3fn_x4")
    SCRATCH["qs%d" % _k] = ("sbuf", [128, W], "uint8")
    SCRATCH["lc%d" % _k] = ("sbuf", [128, W], "float8_e4m3fn_x4")
    SCRATCH["ls%d" % _k] = ("sbuf", [128, W], "uint8")

SEMAPHORES = ["picks", "both", "sent", "mm0", "mm1", "cp0", "cp1", "st0", "st1"]
for _k in range(N):
    SEMAPHORES += ["zt%d" % _k, "vc%d" % _k, "sc%d" % _k, "q%d" % _k, "arr%d" % _k]
    for _u in range(2):
        SEMAPHORES += ["z%d%d" % (_k, _u), "ga%d%d" % (_k, _u), "gx%d%d" % (_k, _u)]


def destinations(rank, T, topo):
    me = T.cores[rank]
    far = lambda r: topo.chip(T.cores[r]) != topo.chip(me)
    other = lambda r: topo.die(T.cores[r]) != topo.die(me)
    return sorted([r for r in range(N) if r != rank], key=lambda r: (not far(r), other(r), r))


def mask_for(core, dst, T, topo):
    if topo.chip(core) != topo.chip(dst):
        return topo.mask(core, dst), len(topo.engines(core, dst))
    leave = set()
    for c in T.cores:
        if topo.chip(c) != topo.chip(core):
            leave |= set(topo.engines(core, c))
    eng = [e for e in topo.engines(core, dst) if e not in leave]
    return sum(1 << e for e in eng), len(eng)


def rank_program(g, core, T, topo):
    rank = T.rank_of(core)
    if rank is None:
        return
    S = T.sem
    v, a, sy, te = g.vector, g.scalar, g.sync, g.tensor
    COPY = ActivationFunctionType.Copy
    dests = destinations(rank, T, topo)
    order = dests + [rank]

    sy.dma_start(T.idx[0:64, 0:16], T.pick[0:64, 0:16]).then_inc(S.picks, 16)
    a.dma_start(T.idx[64:128, 0:14], T.pick[0:64, 2:16]).then_inc(S.picks, 16)
    sy.dma_start(T.xd[:, 0:GW], T.dy[:]).then_inc(S.both, 16)
    a.dma_start(T.xd[:, GW:RW], T.x[:]).then_inc(S.both, 16)

    for k in range(N):
        for u in range(2):
            v.memset(T["dg%d%d" % (k, u)][:], 0.0).then_inc(S["z%d%d" % (k, u)], 1)

    def tile_zeros(k):
        t = T["tile%d" % k]
        v.memset(t[64:128, 0:4 * G0], 0.0).then_inc(S["zt%d" % k], 1)
        v.memset(t[0:64, 4 * X1:4 * W], 0.0).then_inc(S["zt%d" % k], 1)

    def gather(k, u, dst, src, sem):
        c = 4 * order[k] + u
        g.indirect_dma_start(dst, None, src[:], IndirectOffsetOnAxis(ap=T.idx[:, c:c + 1], axis=0),
                             bounds_check=ROWS - 1, oob_is_err=False).then_inc(S[sem], 16)

    def gathers(k):
        if k == 0:
            for u in range(2):
                g.wait_ge(S["z%d%d" % (k, u)], 1)
                gather(k, u, T["dg%d%d" % (k, u)][:, 0:GW], T.dy, "ga%d%d" % (k, u))
            for u in range(2):
                gather(k, u, T["dg%d%d" % (k, u)][:, GW:RW], T.x, "gx%d%d" % (k, u))
        else:
            if k == 1:
                g.wait_ge(S.both, 32)
            for u in range(2):
                g.wait_ge(S["z%d%d" % (k, u)], 1)
                gather(k, u, T["dg%d%d" % (k, u)][:], T.xd, "ga%d%d" % (k, u))

    def build(k):
        t = T["tile%d" % k]
        nv, na = [0], [0]

        def vcopy(out, in_):
            v.tensor_copy(out, in_).then_inc(S["vc%d" % k], 1)
            nv[0] += 1

        def acopy(out, in_):
            a.activation(out, in_, COPY).then_inc(S["sc%d" % k], 1)
            na[0] += 1

        halves = ((0, 64), (64, 128))
        for u in range(2):
            d = T["dg%d%d" % (k, u)]
            v.wait_ge(S["ga%d%d" % (k, u)], 16)
            a.wait_ge(S["ga%d%d" % (k, u)], 16)
            for h in range(2):
                lo, hi = halves[h]
                e = u + 2 * h
                last = HALF if k == 0 else RW - HALF
                vcopy(t[64:128, 4 * G0 + e:4 * (G0 + last):4], d[lo:hi, HALF:HALF + last])
                (acopy if h == 0 else vcopy)(t[0:64, 4 * G0 + e:4 * X1:4], d[lo:hi, 0:HALF])
                if k:
                    acopy(t[0:64, e:4 * G0:4], d[lo:hi, GW:RW])
        if k == 0:
            for u in range(2):
                d = T["dg%d%d" % (k, u)]
                v.wait_ge(S["gx%d%d" % (k, u)], 16)
                a.wait_ge(S["gx%d%d" % (k, u)], 16)
                for h in range(2):
                    lo, hi = halves[h]
                    e = u + 2 * h
                    vcopy(t[64:128, 4 * X1 + e:4 * W:4], d[lo:hi, GW:RW])
                    acopy(t[0:64, e:4 * G0:4], d[lo:hi, GW:RW])
        v.wait_ge(S["zt%d" % k], 2)
        v.wait_ge(S["vc%d" % k], nv[0])
        v.wait_ge(S["sc%d" % k], na[0])
        for j in range(0, W, W // 2):
            b = j + W // 2
            v.quantize_mx(T["qc%d" % k][:, j:b], T["qs%d" % k][:, j:b], t[:, 4 * j:4 * b]).then_inc(S["q%d" % k], 1)

    for k in range(N):
        tile_zeros(k)
        build(k)

    sent = [0]

    def send(k):
        dst = T.cores[order[k]]
        rid, pid, _ = topo.addr(dst)
        m, n = mask_for(core, dst, T, topo)
        g.wait_ge(S["q%d" % k], 2)
        g.remote_dma(T["lc%d" % rank][:].bitcast(dt.uint8), T["qc%d" % k][:].bitcast(dt.uint8),
                     remote_sem=S["arr%d" % rank], local_sem=S.sent, pid=pid, routing_id=rid, dma_engine_mask=m)
        g.remote_dma(T["ls%d" % rank][:], T["qs%d" % k][:],
                     remote_sem=S["arr%d" % rank], local_sem=S.sent, pid=pid, routing_id=rid, dma_engine_mask=m)
        sent[0] += 2 * n

    g.wait_ge(S.picks, 32)
    gathers(0)
    gathers(1)
    send(0)
    gathers(2)
    send(1)
    gathers(3)
    send(2)
    g.wait_ge(S.sent, sent[0])

    place = lambda s: destinations(s, T, topo).index(rank)
    srcs = sorted([s for s in range(N) if s != rank], key=place)
    srcs = srcs[:2] + [rank] + srcs[2:]
    for i, s in enumerate(srcs):
        if s == rank:
            te.wait_ge(S["q%d" % (N - 1)], 2)
            c, z = T["qc%d" % (N - 1)], T["qs%d" % (N - 1)]
        else:
            te.wait_ge(S["arr%d" % s], 2 * mask_for(T.cores[s], core, T, topo)[1])
            c, z = T["lc%d" % s], T["ls%d" % s]
        for b, x in ((0, 0), (1, X1)):
            te.matmul_mx(T["p%d" % b][:], c[:, x:x + XW], z[:, x:x + XW], c[:, G0:X1], z[:, G0:X1],
                         i == 0, i == N - 1).then_inc(S["mm%d" % b], 1)

    v.wait_ge(S.mm0, N)
    v.tensor_copy(T.o0[:], T.p0[:]).then_inc(S.cp0, 1)
    sy.wait_ge(S.cp0, 1)
    sy.dma_start(T.y[:, 0:HALF], T.o0[:]).then_inc(S.st0, 16)
    a.wait_ge(S.mm1, N)
    a.activation(T.o1[:], T.p1[:], COPY).then_inc(S.cp1, 1)
    a.wait_ge(S.cp1, 1)
    a.dma_start(T.y[:, HALF:GW], T.o1[:]).then_inc(S.st1, 16)
    sy.wait_ge(S.st0, 16)
    a.wait_ge(S.st1, 16)
